import numpy as np
import ml_dtypes


def mxq(x, axis, fmt="e4m3"):
    dtype, down = {"e4m3": (ml_dtypes.float8_e4m3fn, 7), "e5m2": (ml_dtypes.float8_e5m2, 14)}[fmt]
    v = np.moveaxis(np.asarray(x, np.float32).astype(ml_dtypes.bfloat16).astype(np.float64), axis, -1)
    blocks = v.reshape(v.shape[:-1] + (-1, 32))
    amax = np.abs(blocks).max(-1, keepdims=True)
    byte = np.maximum(np.where(amax > 0, np.frexp(amax)[1] - 1 + 127, 0) - down, 1)
    scale = np.exp2(byte - 127.0)
    codes = (blocks / scale).astype(np.float32).astype(dtype).astype(np.float64)
    return np.moveaxis((codes * scale).reshape(v.shape), -1, axis)


WIDE = False


def mx_kscale(k):
    if not WIDE:
        return np.ones(k)
    levels = np.array([10, -10, 5, -5, 0])
    if k % 512:
        return np.exp2(np.random.permutation(np.resize(levels, k // 32))).repeat(32)
    a = np.empty((k // 512, 16))
    for p in range(k // 512):
        a[p, :8] = np.random.permutation(np.resize(levels, 8))
        for g in range(8):
            far = levels[np.abs(levels - a[p, g]) >= 10]
            a[p, g + 8] = far[np.random.randint(len(far))]
    return np.exp2(a.ravel()).repeat(32)


def f64(x):
    return np.asarray(x).astype(np.float64)


def striped(idx):
    return np.tile(np.asarray(idx).reshape(-1, 16).T, (8, 1)).astype(np.uint16)


def unstriped(offs):
    return offs[:16].T.reshape(-1).astype(np.int64)


E2M1 = np.array([0.0, 0.5, 1.0, 1.5, 2.0, 3.0, 4.0, 6.0, -0.0, -0.5, -1.0, -1.5, -2.0, -3.0, -4.0, -6.0])


def pack_weight(w, fmt):
    k, n = w.shape
    w = f64(np.asarray(w, np.float32).astype(ml_dtypes.bfloat16)).reshape(k // 32, 32, n)
    amax = np.abs(w).max(1)
    if fmt == "e4m3":
        byte = np.frexp(amax)[1] - 1 + 127 - 7
    else:
        mant, ex = np.frexp(amax / 6.0)
        byte = np.where(mant > 0.5, ex, ex - 1) + 127
    byte = np.clip(np.where(amax > 0, byte, 1), 1, 254)
    scaled = (w * np.exp2(127.0 - byte)[:, None, :]).reshape(k, n).astype(np.float32)
    by_word = np.ascontiguousarray(scaled.reshape(k // 512, 128, 4, n).transpose(0, 1, 3, 2))
    if fmt == "e4m3":
        words = by_word.astype(ml_dtypes.float8_e4m3fn).view(np.uint8)
    else:
        c = by_word.astype(ml_dtypes.float4_e2m1fn).view(np.uint8) & 0xF
        words = (c[..., 0::2] | (c[..., 1::2] << 4)).reshape(k // 512, 128, 2 * n)
    return np.ascontiguousarray(words), np.ascontiguousarray(byte.astype(np.uint8).reshape(k // 512, 16, n))


def unpack_weight(words, scales, fmt):
    g, _, n = scales.shape
    words = np.ascontiguousarray(words).reshape(g, 128, n, -1)
    if fmt == "e4m3":
        vals = words.view(ml_dtypes.float8_e4m3fn).astype(np.float64)
    else:
        nib = np.empty((g, 128, n, 4), np.uint8)
        nib[..., 0::2] = words & 0xF
        nib[..., 1::2] = words >> 4
        vals = E2M1[nib]
    vals = vals * np.repeat(np.exp2(scales.astype(np.float64) - 127.0), 8, axis=1)[..., None]
    return vals.transpose(0, 1, 3, 2).reshape(g * 512, n)


D, T, I, Q, E, K = 512, 2048, 512, 512, 512, 64


def setup_inputs():
    n = np.random.standard_normal
    idx = np.random.permutation(T)[:I]
    fd = mx_kscale(D)
    fi = mx_kscale(I)
    ti = np.ones(T)
    ti[idx] = fi
    keysp = pack_weight(n((D, T)) / fd[:, None], "e4m3")
    return {
        "query": (n((D, Q)) * 1.0 / np.sqrt(D) * fd[:, None]).astype(np.float32),
        "keys_words": keysp[0],
        "keys_scales": keysp[1],
        "lowend": np.tile(np.random.uniform(-1.5, 0.0, T), (128, 1)).astype(np.float32),
        "highend": np.tile(np.random.uniform(0.0, 1.5, T), (128, 1)).astype(np.float32),
        "lam": (np.random.uniform(0.8, 2.0, (Q, 1))).astype(np.float32),
        "pull": (np.random.uniform(0.3, 0.9, (Q, 1))).astype(np.float32),
        "os": (np.random.uniform(4.0, 16.0, (1, I)) * fi).astype(np.float32),
        "vals": (n((E, T)) / ti).astype(np.float32),
        "caution": (np.random.uniform(0.2, 0.8, (1, K))).astype(np.float32),
        "offs": striped(idx),
    }


def reference(query, keys_words, keys_scales, lowend, highend, lam, pull, os, vals, caution, offs):
    idx = unstriped(offs)
    keysu = unpack_weight(keys_words, keys_scales, "e4m3")
    queryq = mxq(f64(query), 0, "e4m3")
    keysidxg = keysu[:, idx]
    a = queryq.T @ keysidxg
    s = np.minimum(a - f64(lowend)[:1][:, idx], f64(highend)[:1][:, idx] - a) * f64(lam)
    p = np.exp(s - np.max(s, axis=1, keepdims=True))
    r = p / np.sum(p, axis=1, keepdims=True)
    r1 = np.pad(r, ((0, 0), (1, 0)))[:, :I]
    w = r - r1 * f64(pull)
    wo1 = w * f64(os)
    wt1 = wo1.T
    vt1 = f64(vals)[:, idx].T
    vt1q = mxq(vt1, 0, "e4m3")
    wt1q = mxq(wt1, 0, "e4m3")
    o = vt1q.T @ wt1q
    y = o.reshape(E, K, Q // K).max(axis=2) - o.reshape(E, K, Q // K).mean(axis=2) * f64(caution)
    return y

@@ -1,0 +1,245 @@
+from contextlib import ExitStack
+
+import concourse.mybir as mybir
+from concourse.masks import make_identity
+
+D, T, I, Q, E, K = 512, 2048, 512, 512, 512, 64
+P = 128
+PACK = 4
+GROUP = Q // K
+HALF = Q // 2
+LEAD = 4
+ROW0 = P - 12
+FLOPS = 2 * D * I * Q + 2 * I * E * Q
+
+F32 = mybir.dt.float32
+BF16 = mybir.dt.bfloat16
+U32 = mybir.dt.uint32
+I32 = mybir.dt.int32
+U16 = mybir.dt.uint16
+U8 = mybir.dt.uint8
+FP8X4 = mybir.dt.float8_e4m3fn_x4
+ALU = mybir.AluOpType
+ACT = mybir.ActivationFunctionType
+AX = mybir.AxisListType
+
+
+def tile_attend_interval_stepwise_groupbestread_kernel(
+    tc, query, keys_words, keys_scales, lowend, highend, lam, pull, slot_factor, vals, caution, offs, out
+):
+    nc = tc.nc
+    with ExitStack() as ctx:
+        sb = ctx.enter_context(tc.tile_pool(name="sb", bufs=1))
+        ps = ctx.enter_context(tc.psum_pool(name="ps", bufs=1))
+
+        def turn(dst, src, start, stop):
+            nc.tensor.matmul(dst, lhsT=src, rhs=ident[:], start=start, stop=stop, is_transpose=True)
+
+        offsets = sb.tile([P, I // 16], U16, name="offsets")
+        nc.sync.dma_start(offsets[:], offs)
+        low_pool = sb.tile([P, T], F32, name="low_pool")
+        nc.vector.memset(low_pool[: P - 2, :], 0.0)
+        nc.sync.dma_start(low_pool[P - 2 :, :], lowend[0:2, :])
+        high_pool = sb.tile([P, T], F32, name="high_pool")
+        nc.vector.memset(high_pool[: P - 1, :], 0.0)
+        nc.sync.dma_start(high_pool[P - 1 :, :], highend[0:1, :])
+        scale_pool = sb.tile([P, T], U8, name="scale_pool")
+        for quad in range(4):
+            rows = keys_scales[0, 4 * quad : 4 * quad + 4, :].bitcast(I32)
+            nc.sync.dma_start(
+                scale_pool[32 * quad : 32 * quad + 32, :].bitcast(I32),
+                rows.unsqueeze(0).to_broadcast([8, 4, T // 4]),
+            )
+        key_pool = sb.tile([P, T], I32, name="key_pool")
+        nc.sync.dma_start(key_pool[:], keys_words[0].rearrange("p n t -> p (n t)").bitcast(I32))
+        q_rows = query.rearrange("(p t) q -> p t q", t=PACK)
+        q_raw = [sb.tile([P, PACK, HALF], F32, name="q_raw%d" % h) for h in range(2)]
+        nc.sync.dma_start(q_raw[0][:], q_rows[:, :, :HALF])
+        nc.sync.dma_start(q_raw[1][:], q_rows[:, :, HALF:])
+        vectors = sb.tile([P, P], F32, name="vectors")
+        nc.gpsimd.memset(vectors[:ROW0, :], 0.0)
+        nc.sync.dma_start(vectors[ROW0 : ROW0 + 4, :], lam.rearrange("(j p) o -> j (p o)", p=P))
+        nc.sync.dma_start(vectors[ROW0 + 4 : ROW0 + 8, :], pull.rearrange("(j p) o -> j (p o)", p=P))
+        nc.sync.dma_start(vectors[ROW0 + 8 :, :], slot_factor.rearrange("o (j p) -> (o j) p", p=P))
+        val_pool = []
+        for e in range(4):
+            pool_e = sb.tile([P, T], F32, name="val_pool%d" % e)
+            nc.sync.dma_start(pool_e[:], vals[e * P : (e + 1) * P, :])
+            val_pool.append(pool_e)
+        caution_b = sb.tile([P, K], F32, name="caution_b")
+        nc.sync.dma_start(caution_b[:], caution.partition_broadcast(P))
+
+        ident = sb.tile([P, P], F32, name="ident")
+        make_identity(nc, ident[:])
+        prob = sb.tile([P, 4, LEAD + I], F32, name="prob")
+        nc.gpsimd.memset(prob[:, :, LEAD - 1 : LEAD], 0.0)
+
+        low_g = sb.tile([P, I], F32, name="low_g")
+        nc.scalar.activation(low_g[:], low_pool[:].indirect(offsets[:]), ACT.Copy)
+        high_g = sb.tile([P, I], F32, name="high_g")
+        nc.scalar.activation(high_g[:], high_pool[:].indirect(offsets[:]), ACT.Copy)
+        key_scales = sb.tile([P, I], U8, name="key_scales", align_bytes=64)
+        nc.vector.tensor_copy(key_scales[:], scale_pool[:].indirect(offsets[:]))
+        key_codes = sb.tile([P, I], U32, name="key_codes", align_bytes=64)
+        nc.vector.tensor_copy(key_codes[:], key_pool[:].bitcast(U32).indirect(offsets[:]))
+
+        ends_t = ps.tile([P, 4, P], F32, name="ends_t", tag="turned", bufs=2)
+        for j in range(4):
+            turn(ends_t[:, j, :], low_g[:, j * P : (j + 1) * P], j == 0, False)
+        for j in range(4):
+            turn(ends_t[:, j, :], high_g[:, j * P : (j + 1) * P], False, j == 3)
+
+        q_codes = sb.tile([P, Q], U32, name="q_codes", align_bytes=64)
+        q_scales = sb.tile([P, Q], U8, name="q_scales", align_bytes=64)
+        neg_mid = sb.tile([P, 4], F32, name="neg_mid")
+        neg_half = sb.tile([P, 4], F32, name="neg_half")
+
+        def queries(h):
+            cols = slice(h * HALF, (h + 1) * HALF)
+            q_bf = sb.tile([P, HALF, PACK], BF16, name="q_bf%d" % h, align_bytes=64)
+            nc.vector.tensor_copy(
+                q_bf[:].rearrange("p (c i) t -> p c t i", i=4),
+                q_raw[h][:].rearrange("p t (c i) -> p c t i", i=4),
+            )
+            nc.vector.quantize_mx(q_codes[:, cols].bitcast(FP8X4), q_scales[:, cols], q_bf[:].rearrange("p q t -> p (q t)"))
+
+        queries(0)
+        nc.vector.tensor_scalar(neg_mid[:], ends_t[:, :, P - 1], -0.5, None, ALU.mult)
+        nc.vector.tensor_tensor(neg_half[:], ends_t[:, :, P - 2], neg_mid[:], ALU.add)
+        vectors_t = ps.tile([P, P], F32, name="vectors_t", tag="turned", bufs=2)
+        turn(vectors_t[:], vectors[:], True, True)
+        columns = sb.tile([P, 12], F32, name="columns")
+        nc.scalar.copy(columns[:], vectors_t[:, ROW0:])
+        neg_pull = sb.tile([P, 4], F32, name="neg_pull")
+        nc.scalar.mul(neg_pull[:], vectors_t[:, ROW0 + 4 : ROW0 + 8], -1.0)
+        factor_row = ps.tile([P, I], F32, name="factor_row")
+        for j in range(4):
+            turn(factor_row[:, j * P : (j + 1) * P], columns[:, 8 + j : 9 + j].to_broadcast([P, P]), True, True)
+
+        queries(1)
+
+        w_codes = sb.tile([P, Q], U32, name="w_codes", align_bytes=64)
+        w_scales = sb.tile([P, Q], U8, name="w_scales", align_bytes=64)
+        v_codes = sb.tile([P, E], U32, name="v_codes", align_bytes=64)
+        v_scales = sb.tile([P, E], U8, name="v_scales", align_bytes=64)
+        held = {}
+
+        def products(b):
+            cols = slice(b * P, (b + 1) * P)
+            bank = ps.tile([P, 4, P], F32, name="product", tag="mx", bufs=2)
+            for j in range(4):
+                slots = slice(j * P, (j + 1) * P)
+                nc.tensor.matmul_mx(
+                    bank[:, j, :],
+                    lhsT=key_codes[:, slots].bitcast(FP8X4),
+                    lhsT_scale=key_scales[:, slots],
+                    rhs=q_codes[:, cols].bitcast(FP8X4),
+                    rhs_scale=q_scales[:, cols],
+                    start=True,
+                    stop=True,
+                )
+            dist = sb.tile([P, 4, P], F32, name="dist%d" % b)
+            for j in range(4):
+                nc.scalar.activation(dist[:, j, :], bank[:, j, :], ACT.Abs, bias=neg_mid[:, j : j + 1])
+            held[b] = dist
+
+        def scores(b):
+            bank = ps.tile([P, I], F32, name="margin", tag="margin", bufs=3)
+            for j in range(4):
+                turn(bank[:, j * P : (j + 1) * P], neg_half[:, j : j + 1].to_broadcast([P, P]), j == 0, False)
+            for j in range(4):
+                turn(bank[:, j * P : (j + 1) * P], held[b][:, j, :], False, j == 3)
+            neg_s = sb.tile([P, I], F32, name="neg_s%d" % b, tag="rows%d" % b)
+            neg_max = sb.tile([P, 1], F32, name="neg_max%d" % b)
+            nc.vector.tensor_scalar(
+                neg_s[:], bank[:], columns[:, b : b + 1], None, ALU.mult, ALU.min, accum_out=neg_max[:]
+            )
+            total = sb.tile([P, 1], F32, name="total%d" % b)
+            nc.scalar.activation(
+                prob[:, b, LEAD:], neg_s[:], ACT.Exp, bias=neg_max[:], scale=-1.0, accum_out=total[:]
+            )
+            held[b] = total
+
+        def to_partitions(rows_bf, codes, scales, name):
+            words = rows_bf.bitcast(F32)
+            bank = ps.tile([P, 2, P], F32, name=name + "_t", tag="turned", bufs=2)
+            for u in range(2):
+                turn(bank[:, u, :], words[:, u::2], True, True)
+            woven = sb.tile([P, P * PACK], BF16, name=name + "_woven", align_bytes=64)
+            nc.scalar.copy(woven[:].bitcast(F32).rearrange("p (c u) -> p c u", u=2), bank[:].rearrange("p u c -> p c u"))
+            nc.vector.quantize_mx(codes.bitcast(FP8X4), scales, woven[:])
+
+        def weights(b):
+            step = sb.tile([P, I], F32, name="step%d" % b)
+            inv = sb.tile([P, 1], F32, name="inv%d" % b)
+            nc.vector.reciprocal(inv[:], held[b][:])
+            nc.vector.scalar_tensor_tensor(
+                step[:], prob[:, b, LEAD - 1 : LEAD - 1 + I], neg_pull[:, b : b + 1], prob[:, b, LEAD:], ALU.mult, ALU.add
+            )
+            w_bf = sb.tile([P, I], BF16, name="w_bf%d" % b)
+            nc.vector.scalar_tensor_tensor(w_bf[:], step[:], inv[:], factor_row[:], ALU.mult, ALU.mult)
+            cols = slice(b * P, (b + 1) * P)
+            to_partitions(w_bf[:], w_codes[:, cols], w_scales[:, cols], "w%d" % b)
+
+        def values(e):
+            v_bf = sb.tile([P, I], BF16, name="v_bf%d" % e, tag="rows%d" % e)
+            nc.scalar.activation(v_bf[:], val_pool[e][:].indirect(offsets[:]), ACT.Copy)
+            cols = slice(e * P, (e + 1) * P)
+            to_partitions(v_bf[:], v_codes[:, cols], v_scales[:, cols], "v%d" % e)
+
+        best = sb.tile([P, 4, K], F32, name="best")
+        sums = sb.tile([P, 4, K], F32, name="sums")
+        result = sb.tile([P, 4, K], F32, name="result")
+        neg_caution = sb.tile([P, K], F32, name="neg_caution")
+        nc.gpsimd.tensor_scalar(neg_caution[:], caution_b[:], -1.0 / GROUP, 0.0, ALU.mult, ALU.add)
+
+        def read(e0, n_e, q0, n_q):
+            bank = ps.tile([P, n_e, n_q], F32, name="read", tag="mx", bufs=2)
+            cols = slice(q0, q0 + n_q)
+            for ee in range(n_e):
+                feats = slice((e0 + ee) * P, (e0 + ee + 1) * P)
+                nc.tensor.matmul_mx(
+                    bank[:, ee, :],
+                    lhsT=v_codes[:, feats].bitcast(FP8X4),
+                    lhsT_scale=v_scales[:, feats],
+                    rhs=w_codes[:, cols].bitcast(FP8X4),
+                    rhs_scale=w_scales[:, cols],
+                    start=True,
+                    stop=True,
+                )
+            grouped = bank[:].rearrange("p e (k g) -> p e k g", g=GROUP)
+            ks = slice(q0 // GROUP, (q0 + n_q) // GROUP)
+            nc.vector.tensor_reduce(sums[:, e0 : e0 + n_e, ks], grouped, AX.X, ALU.add)
+            nc.vector.tensor_reduce(best[:, e0 : e0 + n_e, ks], grouped, AX.X, ALU.max)
+
+        def finish(e0, n_e):
+            es = slice(e0, e0 + n_e)
+            nc.vector.tensor_tensor(
+                sums[:, es, :], sums[:, es, :], neg_caution[:].unsqueeze(1).to_broadcast([P, n_e, K]), ALU.mult
+            )
+            nc.vector.tensor_tensor(result[:, es, :], sums[:, es, :], best[:, es, :], ALU.add)
+            nc.sync.dma_start(out.rearrange("(e p) k -> p e k", p=P)[:, es, :], result[:, es, :])
+
+        products(0)
+        products(1)
+        scores(0)
+        products(2)
+        scores(1)
+        products(3)
+        weights(0)
+        scores(2)
+        values(0)
+        weights(1)
+        scores(3)
+        values(1)
+        weights(2)
+        values(2)
+        weights(3)
+        read(0, 2, 0, HALF)
+        values(3)
+        read(0, 2, HALF, HALF)
+        finish(0, 2)
+        read(2, 1, 0, Q)
+        finish(2, 1)
+        read(3, 1, 0, Q)
+        finish(3, 1)

@@ -37,12 +37,12 @@ def tile_attend_interval_stepwise_groupbestread_kernel(
 
         offsets = sb.tile([P, I // 16], U16, name="offsets")
         nc.sync.dma_start(offsets[:], offs)
+        high_pool = sb.tile([P, T], F32, name="high_pool")
+        nc.gpsimd.memset(high_pool[: P - 1, :], 0.0)
+        nc.sync.dma_start(high_pool[P - 1 :, :], highend[0:1, :])
         low_pool = sb.tile([P, T], F32, name="low_pool")
         nc.vector.memset(low_pool[: P - 2, :], 0.0)
         nc.sync.dma_start(low_pool[P - 2 :, :], lowend[0:2, :])
-        high_pool = sb.tile([P, T], F32, name="high_pool")
-        nc.vector.memset(high_pool[: P - 1, :], 0.0)
-        nc.sync.dma_start(high_pool[P - 1 :, :], highend[0:1, :])
         scale_pool = sb.tile([P, T], U8, name="scale_pool")
         for quad in range(4):
             rows = keys_scales[0, 4 * quad : 4 * quad + 4, :].bitcast(I32)
@@ -52,15 +52,15 @@ def tile_attend_interval_stepwise_groupbestread_kernel(
             )
         key_pool = sb.tile([P, T], I32, name="key_pool")
         nc.sync.dma_start(key_pool[:], keys_words[0].rearrange("p n t -> p (n t)").bitcast(I32))
-        q_rows = query.rearrange("(p t) q -> p t q", t=PACK)
-        q_raw = [sb.tile([P, PACK, HALF], F32, name="q_raw%d" % h) for h in range(2)]
-        nc.sync.dma_start(q_raw[0][:], q_rows[:, :, :HALF])
-        nc.sync.dma_start(q_raw[1][:], q_rows[:, :, HALF:])
         vectors = sb.tile([P, P], F32, name="vectors")
         nc.gpsimd.memset(vectors[:ROW0, :], 0.0)
         nc.sync.dma_start(vectors[ROW0 : ROW0 + 4, :], lam.rearrange("(j p) o -> j (p o)", p=P))
         nc.sync.dma_start(vectors[ROW0 + 4 : ROW0 + 8, :], pull.rearrange("(j p) o -> j (p o)", p=P))
         nc.sync.dma_start(vectors[ROW0 + 8 :, :], slot_factor.rearrange("o (j p) -> (o j) p", p=P))
+        q_rows = query.rearrange("(p t) q -> p t q", t=PACK)
+        q_raw = [sb.tile([P, PACK, HALF], F32, name="q_raw%d" % h) for h in range(2)]
+        nc.sync.dma_start(q_raw[0][:], q_rows[:, :, :HALF])
+        nc.sync.dma_start(q_raw[1][:], q_rows[:, :, HALF:])
         val_pool = []
         for e in range(4):
             pool_e = sb.tile([P, T], F32, name="val_pool%d" % e)
@@ -74,14 +74,12 @@ def tile_attend_interval_stepwise_groupbestread_kernel(
         prob = sb.tile([P, 4, LEAD + I], F32, name="prob")
         nc.gpsimd.memset(prob[:, :, LEAD - 1 : LEAD], 0.0)
 
-        low_g = sb.tile([P, I], F32, name="low_g")
-        nc.scalar.activation(low_g[:], low_pool[:].indirect(offsets[:]), ACT.Copy)
         high_g = sb.tile([P, I], F32, name="high_g")
         nc.scalar.activation(high_g[:], high_pool[:].indirect(offsets[:]), ACT.Copy)
+        low_g = sb.tile([P, I], F32, name="low_g")
+        nc.vector.tensor_copy(low_g[:], low_pool[:].indirect(offsets[:]))
         key_scales = sb.tile([P, I], U8, name="key_scales", align_bytes=64)
-        nc.vector.tensor_copy(key_scales[:], scale_pool[:].indirect(offsets[:]))
         key_codes = sb.tile([P, I], U32, name="key_codes", align_bytes=64)
-        nc.vector.tensor_copy(key_codes[:], key_pool[:].bitcast(U32).indirect(offsets[:]))
 
         ends_t = ps.tile([P, 4, P], F32, name="ends_t", tag="turned", bufs=2)
         for j in range(4):
@@ -94,18 +92,11 @@ def tile_attend_interval_stepwise_groupbestread_kernel(
         neg_mid = sb.tile([P, 4], F32, name="neg_mid")
         neg_half = sb.tile([P, 4], F32, name="neg_half")
 
-        def queries(h):
-            cols = slice(h * HALF, (h + 1) * HALF)
-            q_bf = sb.tile([P, HALF, PACK], BF16, name="q_bf%d" % h, align_bytes=64)
-            nc.vector.tensor_copy(
-                q_bf[:].rearrange("p (c i) t -> p c t i", i=4),
-                q_raw[h][:].rearrange("p t (c i) -> p c t i", i=4),
-            )
-            nc.vector.quantize_mx(q_codes[:, cols].bitcast(FP8X4), q_scales[:, cols], q_bf[:].rearrange("p q t -> p (q t)"))
-
-        queries(0)
+        nc.vector.tensor_copy(key_scales[:], scale_pool[:].indirect(offsets[:]))
         nc.vector.tensor_scalar(neg_mid[:], ends_t[:, :, P - 1], -0.5, None, ALU.mult)
         nc.vector.tensor_tensor(neg_half[:], ends_t[:, :, P - 2], neg_mid[:], ALU.add)
+        nc.vector.tensor_copy(key_codes[:], key_pool[:].bitcast(U32).indirect(offsets[:]))
+
         vectors_t = ps.tile([P, P], F32, name="vectors_t", tag="turned", bufs=2)
         turn(vectors_t[:], vectors[:], True, True)
         columns = sb.tile([P, 12], F32, name="columns")
@@ -116,7 +107,15 @@ def tile_attend_interval_stepwise_groupbestread_kernel(
         for j in range(4):
             turn(factor_row[:, j * P : (j + 1) * P], columns[:, 8 + j : 9 + j].to_broadcast([P, P]), True, True)
 
-        queries(1)
+        def queries(b):
+            h, inner = divmod(b, 2)
+            cols = slice(b * P, (b + 1) * P)
+            q_bf = sb.tile([P, P, PACK], BF16, name="q_bf%d" % b, align_bytes=64)
+            nc.vector.tensor_copy(
+                q_bf[:].rearrange("p (c i) t -> p c t i", i=4),
+                q_raw[h][:, :, inner * P : (inner + 1) * P].rearrange("p t (c i) -> p c t i", i=4),
+            )
+            nc.vector.quantize_mx(q_codes[:, cols].bitcast(FP8X4), q_scales[:, cols], q_bf[:].rearrange("p q t -> p (q t)"))
 
         w_codes = sb.tile([P, Q], U32, name="w_codes", align_bytes=64)
         w_scales = sb.tile([P, Q], U8, name="w_scales", align_bytes=64)
@@ -169,21 +168,28 @@ def tile_attend_interval_stepwise_groupbestread_kernel(
             nc.scalar.copy(woven[:].bitcast(F32).rearrange("p (c u) -> p c u", u=2), bank[:].rearrange("p u c -> p c u"))
             nc.vector.quantize_mx(codes.bitcast(FP8X4), scales, woven[:])
 
-        def weights(b):
+        def weights(b, on_pool):
             step = sb.tile([P, I], F32, name="step%d" % b)
             inv = sb.tile([P, 1], F32, name="inv%d" % b)
             nc.vector.reciprocal(inv[:], held[b][:])
-            nc.vector.scalar_tensor_tensor(
-                step[:], prob[:, b, LEAD - 1 : LEAD - 1 + I], neg_pull[:, b : b + 1], prob[:, b, LEAD:], ALU.mult, ALU.add
-            )
+            before, here = prob[:, b, LEAD - 1 : LEAD - 1 + I], prob[:, b, LEAD:]
+            if on_pool:
+                pulled = sb.tile([P, I], F32, name="pulled%d" % b)
+                nc.gpsimd.tensor_scalar(pulled[:], before, neg_pull[:, b : b + 1], 0.0, ALU.mult, ALU.add)
+                nc.gpsimd.tensor_tensor(step[:], pulled[:], here, ALU.add)
+            else:
+                nc.vector.scalar_tensor_tensor(step[:], before, neg_pull[:, b : b + 1], here, ALU.mult, ALU.add)
             w_bf = sb.tile([P, I], BF16, name="w_bf%d" % b)
             nc.vector.scalar_tensor_tensor(w_bf[:], step[:], inv[:], factor_row[:], ALU.mult, ALU.mult)
             cols = slice(b * P, (b + 1) * P)
             to_partitions(w_bf[:], w_codes[:, cols], w_scales[:, cols], "w%d" % b)
 
-        def values(e):
+        def values(e, on_vector):
             v_bf = sb.tile([P, I], BF16, name="v_bf%d" % e, tag="rows%d" % e)
-            nc.scalar.activation(v_bf[:], val_pool[e][:].indirect(offsets[:]), ACT.Copy)
+            if on_vector:
+                nc.vector.tensor_copy(v_bf[:], val_pool[e][:].indirect(offsets[:]))
+            else:
+                nc.scalar.activation(v_bf[:], val_pool[e][:].indirect(offsets[:]), ACT.Copy)
             cols = slice(e * P, (e + 1) * P)
             to_partitions(v_bf[:], v_codes[:, cols], v_scales[:, cols], "v%d" % e)
 
@@ -214,30 +220,35 @@ def tile_attend_interval_stepwise_groupbestread_kernel(
 
         def finish(e0, n_e):
             es = slice(e0, e0 + n_e)
-            nc.vector.tensor_tensor(
+            nc.gpsimd.tensor_tensor(
                 sums[:, es, :], sums[:, es, :], neg_caution[:].unsqueeze(1).to_broadcast([P, n_e, K]), ALU.mult
             )
-            nc.vector.tensor_tensor(result[:, es, :], sums[:, es, :], best[:, es, :], ALU.add)
+            engine = nc.vector if e0 + n_e == 4 else nc.gpsimd
+            engine.tensor_tensor(result[:, es, :], sums[:, es, :], best[:, es, :], ALU.add)
             nc.sync.dma_start(out.rearrange("(e p) k -> p e k", p=P)[:, es, :], result[:, es, :])
 
+        queries(0)
         products(0)
+        queries(1)
         products(1)
         scores(0)
+        queries(2)
         products(2)
         scores(1)
+        queries(3)
         products(3)
-        weights(0)
+        weights(0, False)
         scores(2)
-        values(0)
-        weights(1)
+        weights(1, False)
         scores(3)
-        values(1)
-        weights(2)
-        values(2)
-        weights(3)
+        values(0, False)
+        weights(2, False)
+        values(1, False)
+        weights(3, False)
         read(0, 2, 0, HALF)
-        values(3)
+        values(2, False)
         read(0, 2, HALF, HALF)
+        values(3, False)
         finish(0, 2)
         read(2, 1, 0, Q)
         finish(2, 1)

from contextlib import ExitStack

import concourse.mybir as mybir
from concourse.masks import make_identity

D, T, I, Q, E, K = 512, 2048, 512, 512, 512, 64
P = 128
PACK = 4
GROUP = Q // K
HALF = Q // 2
LEAD = 4
ROW0 = P - 12
FLOPS = 2 * D * I * Q + 2 * I * E * Q

F32 = mybir.dt.float32
BF16 = mybir.dt.bfloat16
U32 = mybir.dt.uint32
I32 = mybir.dt.int32
U16 = mybir.dt.uint16
U8 = mybir.dt.uint8
FP8X4 = mybir.dt.float8_e4m3fn_x4
ALU = mybir.AluOpType
ACT = mybir.ActivationFunctionType
AX = mybir.AxisListType


def tile_attend_interval_stepwise_groupbestread_kernel(
    tc, query, keys_words, keys_scales, lowend, highend, lam, pull, slot_factor, vals, caution, offs, out
):
    nc = tc.nc
    with ExitStack() as ctx:
        sb = ctx.enter_context(tc.tile_pool(name="sb", bufs=1))
        ps = ctx.enter_context(tc.psum_pool(name="ps", bufs=1))

        def turn(dst, src, start, stop):
            nc.tensor.matmul(dst, lhsT=src, rhs=ident[:], start=start, stop=stop, is_transpose=True)

        offsets = sb.tile([P, I // 16], U16, name="offsets")
        nc.sync.dma_start(offsets[:], offs)
        high_pool = sb.tile([P, T], F32, name="high_pool")
        nc.gpsimd.memset(high_pool[: P - 1, :], 0.0)
        nc.sync.dma_start(high_pool[P - 1 :, :], highend[0:1, :])
        low_pool = sb.tile([P, T], F32, name="low_pool")
        nc.vector.memset(low_pool[: P - 2, :], 0.0)
        nc.sync.dma_start(low_pool[P - 2 :, :], lowend[0:2, :])
        scale_pool = sb.tile([P, T], U8, name="scale_pool")
        for quad in range(4):
            rows = keys_scales[0, 4 * quad : 4 * quad + 4, :].bitcast(I32)
            nc.sync.dma_start(
                scale_pool[32 * quad : 32 * quad + 32, :].bitcast(I32),
                rows.unsqueeze(0).to_broadcast([8, 4, T // 4]),
            )
        key_pool = sb.tile([P, T], I32, name="key_pool")
        nc.sync.dma_start(key_pool[:], keys_words[0].rearrange("p n t -> p (n t)").bitcast(I32))
        vectors = sb.tile([P, P], F32, name="vectors")
        nc.gpsimd.memset(vectors[:ROW0, :], 0.0)
        nc.sync.dma_start(vectors[ROW0 : ROW0 + 4, :], lam.rearrange("(j p) o -> j (p o)", p=P))
        nc.sync.dma_start(vectors[ROW0 + 4 : ROW0 + 8, :], pull.rearrange("(j p) o -> j (p o)", p=P))
        nc.sync.dma_start(vectors[ROW0 + 8 :, :], slot_factor.rearrange("o (j p) -> (o j) p", p=P))
        q_rows = query.rearrange("(p t) q -> p t q", t=PACK)
        q_raw = [sb.tile([P, PACK, HALF], F32, name="q_raw%d" % h) for h in range(2)]
        nc.sync.dma_start(q_raw[0][:], q_rows[:, :, :HALF])
        nc.sync.dma_start(q_raw[1][:], q_rows[:, :, HALF:])
        val_pool = []
        for e in range(4):
            pool_e = sb.tile([P, T], F32, name="val_pool%d" % e)
            nc.sync.dma_start(pool_e[:], vals[e * P : (e + 1) * P, :])
            val_pool.append(pool_e)
        caution_b = sb.tile([P, K], F32, name="caution_b")
        nc.sync.dma_start(caution_b[:], caution.partition_broadcast(P))

        ident = sb.tile([P, P], F32, name="ident")
        make_identity(nc, ident[:])
        prob = sb.tile([P, 4, LEAD + I], F32, name="prob")
        nc.gpsimd.memset(prob[:, :, LEAD - 1 : LEAD], 0.0)

        high_g = sb.tile([P, I], F32, name="high_g")
        nc.scalar.activation(high_g[:], high_pool[:].indirect(offsets[:]), ACT.Copy)
        low_g = sb.tile([P, I], F32, name="low_g")
        nc.vector.tensor_copy(low_g[:], low_pool[:].indirect(offsets[:]))
        key_scales = sb.tile([P, I], U8, name="key_scales", align_bytes=64)
        key_codes = sb.tile([P, I], U32, name="key_codes", align_bytes=64)

        ends_t = ps.tile([P, 4, P], F32, name="ends_t", tag="turned", bufs=2)
        for j in range(4):
            turn(ends_t[:, j, :], low_g[:, j * P : (j + 1) * P], j == 0, False)
        for j in range(4):
            turn(ends_t[:, j, :], high_g[:, j * P : (j + 1) * P], False, j == 3)

        q_codes = sb.tile([P, Q], U32, name="q_codes", align_bytes=64)
        q_scales = sb.tile([P, Q], U8, name="q_scales", align_bytes=64)
        neg_mid = sb.tile([P, 4], F32, name="neg_mid")
        neg_half = sb.tile([P, 4], F32, name="neg_half")

        nc.vector.tensor_copy(key_scales[:], scale_pool[:].indirect(offsets[:]))
        nc.vector.tensor_scalar(neg_mid[:], ends_t[:, :, P - 1], -0.5, None, ALU.mult)
        nc.vector.tensor_tensor(neg_half[:], ends_t[:, :, P - 2], neg_mid[:], ALU.add)
        nc.vector.tensor_copy(key_codes[:], key_pool[:].bitcast(U32).indirect(offsets[:]))

        vectors_t = ps.tile([P, P], F32, name="vectors_t", tag="turned", bufs=2)
        turn(vectors_t[:], vectors[:], True, True)
        columns = sb.tile([P, 12], F32, name="columns")
        nc.scalar.copy(columns[:], vectors_t[:, ROW0:])
        neg_pull = sb.tile([P, 4], F32, name="neg_pull")
        nc.scalar.mul(neg_pull[:], vectors_t[:, ROW0 + 4 : ROW0 + 8], -1.0)
        factor_row = ps.tile([P, I], F32, name="factor_row")
        for j in range(4):
            turn(factor_row[:, j * P : (j + 1) * P], columns[:, 8 + j : 9 + j].to_broadcast([P, P]), True, True)

        def queries(b):
            h, inner = divmod(b, 2)
            cols = slice(b * P, (b + 1) * P)
            q_bf = sb.tile([P, P, PACK], BF16, name="q_bf%d" % b, align_bytes=64)
            nc.vector.tensor_copy(
                q_bf[:].rearrange("p (c i) t -> p c t i", i=4),
                q_raw[h][:, :, inner * P : (inner + 1) * P].rearrange("p t (c i) -> p c t i", i=4),
            )
            nc.vector.quantize_mx(q_codes[:, cols].bitcast(FP8X4), q_scales[:, cols], q_bf[:].rearrange("p q t -> p (q t)"))

        w_codes = sb.tile([P, Q], U32, name="w_codes", align_bytes=64)
        w_scales = sb.tile([P, Q], U8, name="w_scales", align_bytes=64)
        v_codes = sb.tile([P, E], U32, name="v_codes", align_bytes=64)
        v_scales = sb.tile([P, E], U8, name="v_scales", align_bytes=64)
        held = {}

        def products(b):
            cols = slice(b * P, (b + 1) * P)
            bank = ps.tile([P, 4, P], F32, name="product", tag="mx", bufs=2)
            for j in range(4):
                slots = slice(j * P, (j + 1) * P)
                nc.tensor.matmul_mx(
                    bank[:, j, :],
                    lhsT=key_codes[:, slots].bitcast(FP8X4),
                    lhsT_scale=key_scales[:, slots],
                    rhs=q_codes[:, cols].bitcast(FP8X4),
                    rhs_scale=q_scales[:, cols],
                    start=True,
                    stop=True,
                )
            dist = sb.tile([P, 4, P], F32, name="dist%d" % b)
            for j in range(4):
                nc.scalar.activation(dist[:, j, :], bank[:, j, :], ACT.Abs, bias=neg_mid[:, j : j + 1])
            held[b] = dist

        def scores(b):
            bank = ps.tile([P, I], F32, name="margin", tag="margin", bufs=3)
            for j in range(4):
                turn(bank[:, j * P : (j + 1) * P], neg_half[:, j : j + 1].to_broadcast([P, P]), j == 0, False)
            for j in range(4):
                turn(bank[:, j * P : (j + 1) * P], held[b][:, j, :], False, j == 3)
            neg_s = sb.tile([P, I], F32, name="neg_s%d" % b, tag="rows%d" % b)
            neg_max = sb.tile([P, 1], F32, name="neg_max%d" % b)
            nc.vector.tensor_scalar(
                neg_s[:], bank[:], columns[:, b : b + 1], None, ALU.mult, ALU.min, accum_out=neg_max[:]
            )
            total = sb.tile([P, 1], F32, name="total%d" % b)
            nc.scalar.activation(
                prob[:, b, LEAD:], neg_s[:], ACT.Exp, bias=neg_max[:], scale=-1.0, accum_out=total[:]
            )
            held[b] = total

        def to_partitions(rows_bf, codes, scales, name):
            words = rows_bf.bitcast(F32)
            bank = ps.tile([P, 2, P], F32, name=name + "_t", tag="turned", bufs=2)
            for u in range(2):
                turn(bank[:, u, :], words[:, u::2], True, True)
            woven = sb.tile([P, P * PACK], BF16, name=name + "_woven", align_bytes=64)
            nc.scalar.copy(woven[:].bitcast(F32).rearrange("p (c u) -> p c u", u=2), bank[:].rearrange("p u c -> p c u"))
            nc.vector.quantize_mx(codes.bitcast(FP8X4), scales, woven[:])

        def weights(b, on_pool):
            step = sb.tile([P, I], F32, name="step%d" % b)
            inv = sb.tile([P, 1], F32, name="inv%d" % b)
            nc.vector.reciprocal(inv[:], held[b][:])
            before, here = prob[:, b, LEAD - 1 : LEAD - 1 + I], prob[:, b, LEAD:]
            if on_pool:
                pulled = sb.tile([P, I], F32, name="pulled%d" % b)
                nc.gpsimd.tensor_scalar(pulled[:], before, neg_pull[:, b : b + 1], 0.0, ALU.mult, ALU.add)
                nc.gpsimd.tensor_tensor(step[:], pulled[:], here, ALU.add)
            else:
                nc.vector.scalar_tensor_tensor(step[:], before, neg_pull[:, b : b + 1], here, ALU.mult, ALU.add)
            w_bf = sb.tile([P, I], BF16, name="w_bf%d" % b)
            nc.vector.scalar_tensor_tensor(w_bf[:], step[:], inv[:], factor_row[:], ALU.mult, ALU.mult)
            cols = slice(b * P, (b + 1) * P)
            to_partitions(w_bf[:], w_codes[:, cols], w_scales[:, cols], "w%d" % b)

        def values(e, on_vector):
            v_bf = sb.tile([P, I], BF16, name="v_bf%d" % e, tag="rows%d" % e)
            if on_vector:
                nc.vector.tensor_copy(v_bf[:], val_pool[e][:].indirect(offsets[:]))
            else:
                nc.scalar.activation(v_bf[:], val_pool[e][:].indirect(offsets[:]), ACT.Copy)
            cols = slice(e * P, (e + 1) * P)
            to_partitions(v_bf[:], v_codes[:, cols], v_scales[:, cols], "v%d" % e)

        best = sb.tile([P, 4, K], F32, name="best")
        sums = sb.tile([P, 4, K], F32, name="sums")
        result = sb.tile([P, 4, K], F32, name="result")
        neg_caution = sb.tile([P, K], F32, name="neg_caution")
        nc.gpsimd.tensor_scalar(neg_caution[:], caution_b[:], -1.0 / GROUP, 0.0, ALU.mult, ALU.add)

        def read(e0, n_e, q0, n_q):
            bank = ps.tile([P, n_e, n_q], F32, name="read", tag="mx", bufs=2)
            cols = slice(q0, q0 + n_q)
            for ee in range(n_e):
                feats = slice((e0 + ee) * P, (e0 + ee + 1) * P)
                nc.tensor.matmul_mx(
                    bank[:, ee, :],
                    lhsT=v_codes[:, feats].bitcast(FP8X4),
                    lhsT_scale=v_scales[:, feats],
                    rhs=w_codes[:, cols].bitcast(FP8X4),
                    rhs_scale=w_scales[:, cols],
                    start=True,
                    stop=True,
                )
            grouped = bank[:].rearrange("p e (k g) -> p e k g", g=GROUP)
            ks = slice(q0 // GROUP, (q0 + n_q) // GROUP)
            nc.vector.tensor_reduce(sums[:, e0 : e0 + n_e, ks], grouped, AX.X, ALU.add)
            nc.vector.tensor_reduce(best[:, e0 : e0 + n_e, ks], grouped, AX.X, ALU.max)

        def finish(e0, n_e):
            es = slice(e0, e0 + n_e)
            nc.gpsimd.tensor_tensor(
                sums[:, es, :], sums[:, es, :], neg_caution[:].unsqueeze(1).to_broadcast([P, n_e, K]), ALU.mult
            )
            engine = nc.vector if e0 + n_e == 4 else nc.gpsimd
            engine.tensor_tensor(result[:, es, :], sums[:, es, :], best[:, es, :], ALU.add)
            nc.sync.dma_start(out.rearrange("(e p) k -> p e k", p=P)[:, es, :], result[:, es, :])

        queries(0)
        products(0)
        queries(1)
        products(1)
        scores(0)
        queries(2)
        products(2)
        scores(1)
        queries(3)
        products(3)
        weights(0, False)
        scores(2)
        weights(1, False)
        scores(3)
        values(0, False)
        weights(2, False)
        values(1, False)
        weights(3, False)
        read(0, 2, 0, HALF)
        values(2, False)
        read(0, 2, HALF, HALF)
        values(3, False)
        finish(0, 2)
        read(2, 1, 0, Q)
        finish(2, 1)
        read(3, 1, 0, Q)
        finish(3, 1)
